import numpy as np
import ml_dtypes


def mxq(x, axis, fmt="e4m3"):
    dtype, down = {"e4m3": (ml_dtypes.float8_e4m3fn, 7), "e5m2": (ml_dtypes.float8_e5m2, 14)}[fmt]
    v = np.moveaxis(np.asarray(x, np.float32).astype(ml_dtypes.bfloat16).astype(np.float64), axis, -1)
    blocks = v.reshape(v.shape[:-1] + (-1, 32))
    amax = np.abs(blocks).max(-1, keepdims=True)
    byte = np.maximum(np.where(amax > 0, np.frexp(amax)[1] - 1 + 127, 0) - down, 1)
    scale = np.exp2(byte - 127.0)
    codes = (blocks / scale).astype(np.float32).astype(dtype).astype(np.float64)
    return np.moveaxis((codes * scale).reshape(v.shape), -1, axis)


WIDE = False


def mx_kscale(k):
    if not WIDE:
        return np.ones(k)
    levels = np.array([10, -10, 5, -5, 0])
    if k % 512:
        return np.exp2(np.random.permutation(np.resize(levels, k // 32))).repeat(32)
    a = np.empty((k // 512, 16))
    for p in range(k // 512):
        a[p, :8] = np.random.permutation(np.resize(levels, 8))
        for g in range(8):
            far = levels[np.abs(levels - a[p, g]) >= 10]
            a[p, g + 8] = far[np.random.randint(len(far))]
    return np.exp2(a.ravel()).repeat(32)


def f64(x):
    return np.asarray(x).astype(np.float64)


def striped(idx):
    return np.tile(idx.reshape(-1, 16).T, (8, 1)).astype(np.uint16)


def unstriped(offs):
    return offs[:16].T.reshape(-1).astype(np.int64)


def striped8(idx):
    return np.concatenate([x.reshape(-1, 16).T for x in idx]).astype(np.uint16)


def runs(offs, k):
    lists = np.stack([offs[16 * r : 16 * r + 16].T.reshape(-1) for r in range(8)]).astype(np.int64)
    return lists[np.arange(k) % 512 // 64]


def pack_weight(w):
    k, n = w.shape
    w = f64(np.asarray(w, np.float32).astype(ml_dtypes.bfloat16)).reshape(k // 32, 32, n)
    amax = np.abs(w).max(1)
    byte = np.clip(np.where(amax > 0, np.frexp(amax)[1] - 1 + 127 - 7, 1), 1, 254)
    scaled = (w * np.exp2(127.0 - byte)[:, None, :]).reshape(k, n).astype(np.float32)
    words = np.ascontiguousarray(scaled.reshape(k // 512, 128, 4, n).transpose(0, 1, 3, 2)).astype(ml_dtypes.float8_e4m3fn).view(np.uint8)
    return words, np.ascontiguousarray(byte.astype(np.uint8).reshape(k // 512, 16, n))


def unpack_weight(words, scales):
    g, p, n, _ = words.shape
    vals = np.ascontiguousarray(words).view(ml_dtypes.float8_e4m3fn).astype(np.float64) * np.repeat(np.exp2(scales.astype(np.float64) - 127.0), 8, axis=1)[..., None]
    return vals.transpose(0, 1, 3, 2).reshape(g * 512, n)


E2M1 = np.array([0.0, 0.5, 1.0, 1.5, 2.0, 3.0, 4.0, 6.0, -0.0, -0.5, -1.0, -1.5, -2.0, -3.0, -4.0, -6.0])


def pack_fp4(w):
    k, n = w.shape
    w = f64(np.asarray(w, np.float32).astype(ml_dtypes.bfloat16)).reshape(k // 32, 32, n)
    amax = np.abs(w).max(1)
    mant, ex = np.frexp(amax / 6.0)
    byte = np.clip(np.where(amax > 0, np.where(mant > 0.5, ex, ex - 1) + 127, 1), 1, 254)
    scaled = (w * np.exp2(127.0 - byte)[:, None, :]).reshape(k, n).astype(np.float32)
    c = np.ascontiguousarray(scaled.reshape(k // 512, 128, 4, n).transpose(0, 1, 3, 2)).astype(ml_dtypes.float4_e2m1fn).view(np.uint8) & 0xF
    words = (c[..., 0::2] | (c[..., 1::2] << 4)).reshape(k // 512, 128, 2 * n)
    return np.ascontiguousarray(words), np.ascontiguousarray(byte.astype(np.uint8).reshape(k // 512, 16, n))


def unpack_fp4(words, scales):
    g, _, n = scales.shape
    words = np.ascontiguousarray(words).reshape(g, 128, n, 2)
    nib = np.empty((g, 128, n, 4), np.uint8)
    nib[..., 0::2] = words & 0xF
    nib[..., 1::2] = words >> 4
    vals = E2M1[nib] * np.repeat(np.exp2(scales.astype(np.float64) - 127.0), 8, axis=1)[..., None]
    return vals.transpose(0, 1, 3, 2).reshape(g * 512, n)


def sigmoid(v):
    return 1.0 / (1.0 + np.exp(-np.maximum(v, -700.0)))

def planes(y):
    n, m = y.shape
    v = y.astype(np.float32).astype(ml_dtypes.bfloat16).astype(np.float64).reshape(n // 32, 32, m)
    top = np.abs(v).max(1)
    byte = np.clip(np.where(top > 0, np.frexp(top)[1] - 1 + 127 - 7, 1), 1, 254)
    codes = (v * np.exp2(127.0 - byte)[:, None, :]).reshape(n, m).astype(np.float32).astype(ml_dtypes.float8_e4m3fn).view(np.uint8)
    words = codes.reshape(n // 512, 128, 4, m).transpose(0, 1, 3, 2)
    return np.ascontiguousarray(words), np.ascontiguousarray(byte.astype(np.uint8).reshape(n // 512, 16, m))


K, T, S, V, H = 512, 2048, 512, 256, 512


def setup_inputs():
    n = np.random.standard_normal
    s = mx_kscale(K)[:, None]
    u = mx_kscale(S)
    packed_xT = pack_weight(n((K, T)) * s)
    packed_w1 = pack_fp4(n((K, H)) / np.sqrt(K) / s)
    packed_w2 = pack_fp4(n((K, H)) / np.sqrt(K) / s)
    return {
        "x_words": packed_xT[0],
        "x_scales": packed_xT[1],
        "w1_words": packed_w1[0],
        "w1_scales": packed_w1[1],
        "w2_words": packed_w2[0],
        "w2_scales": packed_w2[1],
        "sl": np.random.uniform(1.0, 2.0, (H, 1)).astype(np.float32),
        "th": (0.5 * n((H, 1))).astype(np.float32),
        "tau": np.random.uniform(0.2, 0.6, (H, 1)).astype(np.float32),
        "tau2": np.random.uniform(0.6, 1.0, (H, 1)).astype(np.float32),
        "ga": (np.random.uniform(0.5, 1.5, (H, 1)) * u[:, None]).astype(np.float32),
        "gb": (np.random.uniform(0.5, 1.5, (H, 1)) / u[:, None]).astype(np.float32),
        "tau3": np.random.uniform(0.3, 0.9, (S, 1)).astype(np.float32),
        "offs": striped8(np.random.randint(0, T, (8, S))),
        "two": striped(np.random.permutation(T)[:V]),
        "n1": striped8(np.stack([np.random.permutation(S) for _ in range(8)])),
        "n2": striped8(np.stack([np.random.permutation(S) for _ in range(8)])),
        "n3": striped8(np.stack([np.random.permutation(V) for _ in range(8)])),
        "n4": striped8(np.stack([np.random.permutation(V) for _ in range(8)])),
        "n5": striped8(np.stack([np.random.permutation(V) for _ in range(8)])),
        "n6": striped8(np.stack([np.random.permutation(V) for _ in range(8)])),
    }


def reference(x_words, x_scales, w1_words, w1_scales, w2_words, w2_scales, sl, th, tau, tau2, ga, gb, tau3, offs, two, n1, n2, n3, n4, n5, n6):
    xq = unpack_weight(x_words, x_scales)[np.arange(K)[:, None], runs(offs, K)]
    a = unpack_fp4(w1_words, w1_scales).T @ xq
    sg = sigmoid(f64(sl) * (a[np.arange(H)[:, None], runs(n1, H)] - f64(th)))
    st = a * sg
    z = f64(ga) * (st - (0.5 * (st[np.arange(H)[:, None], runs(n2, H)])))
    x_two = unpack_weight(x_words, x_scales)[:, unstriped(two)]
    b = unpack_fp4(w2_words, w2_scales).T @ x_two
    top = b.max(axis=1, keepdims=True)
    ea = np.exp(f64(tau) * (b[np.arange(H)[:, None], runs(n3, H)] - top))
    ea2 = np.exp(f64(tau2) * (b[np.arange(H)[:, None], runs(n4, H)] - top))
    z2 = f64(gb) * (3.0 * (ea - ea2))
    s = 0.0625 * ((mxq(z, 0, "e4m3").T @ mxq(z2, 0, "e4m3")))
    top2 = s.max(axis=1, keepdims=True)
    ea3 = np.exp(f64(tau3) * (s[np.arange(S)[:, None], runs(n5, S)] - top2))
    ea4 = np.exp(f64(tau3) * (s[np.arange(S)[:, None], runs(n6, S)] - top2))
    out_0 = s + np.log(ea3 + ea4 + 0.25)
    return (out_0,) + planes(out_0)

@@ -1,0 +1,284 @@
+from contextlib import ExitStack
+
+import concourse.mybir as mybir
+
+K, T, S, V, H = 512, 2048, 512, 256, 512
+FLOPS = 2 * K * H * S + 2 * K * H * V + 2 * H * S * V
+
+F32 = mybir.dt.float32
+BF16 = mybir.dt.bfloat16
+I32 = mybir.dt.int32
+U32 = mybir.dt.uint32
+U16 = mybir.dt.uint16
+U8 = mybir.dt.uint8
+FP8X4 = mybir.dt.float8_e4m3fn_x4
+FP4X4 = mybir.dt.float4_e2m1fn_x4
+ALU = mybir.AluOpType
+ACT = mybir.ActivationFunctionType
+
+P = 128
+R = 4
+
+
+def tile_picked_hkqehpetwelg_none_po_kernel(
+    tc, x_words, x_scales, w1_words, w1_scales, w2_words, w2_scales, sl, th, tau, tau2, ga, gb, tau3,
+    offs, two, n1, n2, n3, n4, n5, n6, out_0, out_1, out_2,
+):
+    nc = tc.nc
+    with ExitStack() as ctx:
+        keep = ctx.enter_context(tc.tile_pool(name="keep", bufs=1))
+        ring = ctx.enter_context(tc.tile_pool(name="ring", bufs=2))
+        stage = ctx.enter_context(tc.tile_pool(name="stage", bufs=1))
+        psum = ctx.enter_context(tc.psum_pool(name="psum", bufs=1))
+
+        def load_list(src, name):
+            dst = keep.tile(list(src.shape), U16, name=name)
+            nc.sync.dma_start(dst[:], src)
+            return dst
+
+        def load_rows(queue, src, name, pool=keep, offset=None):
+            dst = pool.tile([P, R], F32, name=name, offset=offset)
+            queue.dma_start(dst[:], src.rearrange("(p t) o -> p (t o)", t=R))
+            return dst
+
+        def load_weight_scales(dst, src, quadrants):
+            for q in quadrants:
+                rows = src[0][4 * q : 4 * q + 4, :].bitcast(I32)
+                nc.sync.dma_start(dst[32 * q : 32 * q + 32, :].bitcast(I32), rows.unsqueeze(0).to_broadcast([8, 4, H // 4]))
+
+        offs_l = load_list(offs, "offs_l")
+        xs = stage.tile([P, T], U8, name="xs", offset=0)
+        for par in range(2):
+            rows = x_scales[0][par:16:2, :].bitcast(I32)
+            nc.sync.dma_start(xs[par:P:2, :].bitcast(I32), rows.unsqueeze(1).to_broadcast([8, 8, T // 4]))
+        two_l = load_list(two, "two_l")
+        w1w_raw = keep.tile([P, 2 * H], U8, name="w1w_raw")
+        nc.sync.dma_start(w1w_raw[:].bitcast(I32), w1_words[0].bitcast(I32))
+        w1s_raw = keep.tile([P, H], U8, name="w1s_raw")
+        load_weight_scales(w1s_raw, w1_scales, (0, 1))
+        xw = keep.tile([P, T], U32, name="xw")
+        nc.sync.dma_start(xw[:].bitcast(I32), x_words[0].rearrange("p n t -> p (n t)").bitcast(I32))
+        load_weight_scales(w1s_raw, w1_scales, (2, 3))
+        n1_l = load_list(n1, "n1_l")
+        n2_l = load_list(n2, "n2_l")
+        sl_t = load_rows(nc.gpsimd, sl, "sl_t")
+        th_t = load_rows(nc.gpsimd, th, "th_t")
+        n3_l = load_list(n3, "n3_l")
+        n4_l = load_list(n4, "n4_l")
+        n5_l = load_list(n5, "n5_l")
+        n6_l = load_list(n6, "n6_l")
+
+        a_win = [keep.tile([P, 2 * S], F32, name="a_win%d" % t) for t in range(R)]
+        bs_win = [keep.tile([P, 2 * V], F32, name="bs_win%d" % t) for t in range(R)]
+
+        def pick_words(lst, n, name):
+            picked = keep.tile([P, n], U32, name=name, align_bytes=64)
+            nc.vector.tensor_copy(picked[:], xw[:].indirect(lst[:]))
+            return picked
+
+        def deal_words(raw, name):
+            dealt = keep.tile([P, 2 * H], U8, name=name, align_bytes=64)
+            nc.gpsimd.tensor_copy(
+                dealt[:].rearrange("p (t m b) -> p t m b", t=R, b=2),
+                raw[:].rearrange("p (m t b) -> p t m b", t=R, b=2),
+            )
+            return dealt
+
+        def deal_scales(engine, raw, name):
+            dealt = keep.tile([P, H], U8, name=name, align_bytes=64)
+            engine.tensor_copy(
+                dealt[:].rearrange("p (t m) -> p t m", t=R), raw[:].rearrange("p (m t) -> p t m", t=R)
+            )
+            return dealt
+
+        picked_s = keep.tile([P, S + V], U8, name="picked_s", align_bytes=64)
+        nc.vector.tensor_copy(picked_s[:, :S], xs[:].indirect(offs_l[:]))
+        nc.vector.tensor_copy(picked_s[:, S:], xs[:].indirect(two_l[:]))
+        plane_s = keep.tile([P, S + V], U8, name="plane_s", align_bytes=64)
+        nc.vector.tensor_copy(plane_s[:].bitcast(I32), picked_s[:].bitcast(I32))
+        for par in range(2):
+            nc.scalar.dma_start(plane_s[2 + par : P : 32, :].bitcast(I32), picked_s[16 + par : P : 32, :].bitcast(I32))
+        xa_s = plane_s[:, :S]
+        xb_s = plane_s[:, S:]
+        w1w = deal_words(w1w_raw, "w1w")
+        w1s = deal_scales(nc.gpsimd, w1s_raw, "w1s")
+        xa_w = pick_words(offs_l, S, "xa_w")
+        xb_w = pick_words(two_l, V, "xb_w")
+        for t in range(R):
+            nc.vector.memset(a_win[t][:, S:], 0.0)
+            nc.vector.memset(bs_win[t][:, V:], 0.0)
+
+        ga_t = load_rows(nc.sync, ga, "ga_t", stage, 1536)
+        w2w_raw = stage.tile([P, 2 * H], U8, name="w2w_raw", offset=0)
+        nc.sync.dma_start(w2w_raw[:].bitcast(I32), w2_words[0].bitcast(I32))
+        w2s_raw = stage.tile([P, H], U8, name="w2s_raw", offset=1024)
+        load_weight_scales(w2s_raw, w2_scales, range(4))
+        tau_t = load_rows(nc.sync, tau, "tau_t", stage, 1568)
+        tau2_t = load_rows(nc.sync, tau2, "tau2_t", stage, 1600)
+        gb_t = load_rows(nc.sync, gb, "gb_t", stage, 1632)
+        tau3_t = load_rows(nc.sync, tau3, "tau3_t", stage, 1664)
+        w2w = deal_words(w2w_raw, "w2w")
+        w2s = deal_scales(nc.gpsimd, w2s_raw, "w2s")
+
+        sig_bias = stage.tile([P, R], F32, name="sig_bias", offset=1696)
+        nc.vector.scalar_tensor_tensor(sig_bias[:], sl_t[:], -1.0, th_t[:], ALU.mult, ALU.mult)
+        half_ga = keep.tile([P, R], F32, name="half_ga")
+        nc.gpsimd.tensor_scalar(half_ga[:], ga_t[:], -0.5, 0.0, ALU.mult, ALU.add)
+        gb3 = keep.tile([P, R], F32, name="gb3")
+        nc.gpsimd.tensor_scalar(gb3[:], gb_t[:], 3.0, 0.0, ALU.mult, ALU.add)
+
+        def project(bank, words, scales, t, x_w, x_s):
+            nc.tensor.matmul_mx(
+                out=bank,
+                lhsT=words[:, 2 * P * t : 2 * P * (t + 1)].bitcast(FP4X4),
+                lhsT_scale=scales[:, P * t : P * (t + 1)],
+                rhs=x_w[:].bitcast(FP8X4),
+                rhs_scale=x_s,
+                start=True,
+                stop=True,
+            )
+
+        st_win = [keep.tile([P, 2 * S], F32, name="st_win%d" % t) for t in range(R)]
+        z = keep.tile([P, R, S], F32, name="z")
+        whole = [keep.tile([P, S], F32, name="whole%d" % t) for t in range(R)]
+
+        a_plain = []
+
+        def product_a(t):
+            a_ps = psum.tile([P, S], F32, name="a_ps%d" % t, tag="wide%d" % (t % 2))
+            project(a_ps[:], w1w, w1s, t, xa_w, xa_s)
+            if t < 2:
+                nc.vector.tensor_copy(a_win[t][:, :S], a_ps[:])
+                a_plain.append(a_win[t][:, :S])
+            else:
+                nc.scalar.copy(a_win[t][:, :S], a_ps[:])
+                a_plain.append(a_ps[:])
+
+        def gate(t):
+            nc.scalar.activation(
+                st_win[t][:, S:], a_win[t][:].indirect(n1_l[:]), ACT.Sigmoid,
+                bias=sig_bias[:, t : t + 1], scale=sl_t[:, t : t + 1],
+            )
+
+        def weigh(t):
+            nc.vector.scalar_tensor_tensor(
+                st_win[t][:, :S], a_plain[t], half_ga[:, t : t + 1], st_win[t][:, S:], ALU.mult, ALU.mult
+            )
+
+        def double(t):
+            nc.vector.tensor_scalar(whole[t][:], st_win[t][:, :S], -2.0, None, ALU.mult)
+
+        def fetch(t):
+            nc.vector.tensor_tensor(z[:, t, :], st_win[t][:].indirect(n2_l[:]), whole[t][:], ALU.add)
+
+        product_a(0)
+        product_a(1)
+        gate(0)
+        gate(1)
+        product_a(2)
+        gate(2)
+        product_a(3)
+        gate(3)
+
+        weigh(0)
+        double(0)
+        weigh(1)
+        fetch(0)
+        top = keep.tile([P, R], F32, name="top")
+        for t in range(R):
+            b_ps = psum.tile([P, V], F32, name="b_ps%d" % t, tag="narrow%d" % t)
+            project(b_ps[:], w2w, w2s, t, xb_w, xb_s)
+            nc.vector.tensor_scalar(bs_win[t][:, :V], b_ps[:], 1.0, None, ALU.mult, ALU.max, accum_out=top[:, t : t + 1])
+        exp_bias = keep.tile([P, 2, R], F32, name="exp_bias")
+        nc.vector.scalar_tensor_tensor(exp_bias[:, 0, :], top[:], -1.0, tau_t[:], ALU.mult, ALU.mult)
+        nc.vector.scalar_tensor_tensor(exp_bias[:, 1, :], top[:], -1.0, tau2_t[:], ALU.mult, ALU.mult)
+        for t in range(1, R):
+            double(t)
+            if t + 1 < R:
+                weigh(t + 1)
+            fetch(t)
+
+        z_bf = keep.tile([P, R * S], BF16, name="z_bf", align_bytes=64)
+        nc.vector.tensor_copy(
+            z_bf[:].rearrange("p (u m k) -> p m k u", u=R, k=R), z[:].rearrange("p k (m u) -> p m k u", u=R)
+        )
+        z_w = keep.tile([P, S], U32, name="z_w", align_bytes=64)
+        z_s = keep.tile([P, S], U8, name="z_s", align_bytes=64)
+        nc.vector.quantize_mx(out=z_w[:].bitcast(FP8X4), scales=z_s[:], in_=z_bf[:])
+
+        diff = keep.tile([P, R, V], F32, name="diff")
+        eas = keep.tile([P, R, 2, V], F32, name="eas", tag="a_win3")
+        for t in range(R):
+            ea = eas[:, t, 0, :]
+            ea2 = eas[:, t, 1, :]
+            nc.scalar.activation(
+                ea, bs_win[t][:].indirect(n3_l[:]), ACT.Exp, bias=exp_bias[:, 0, t : t + 1], scale=tau_t[:, t : t + 1]
+            )
+            nc.scalar.activation(
+                ea2, bs_win[t][:].indirect(n4_l[:]), ACT.Exp, bias=exp_bias[:, 1, t : t + 1], scale=tau2_t[:, t : t + 1]
+            )
+            nc.vector.tensor_tensor(diff[:, t, :], ea, ea2, ALU.subtract)
+        z2_bf = keep.tile([P, R * V], BF16, name="z2_bf", align_bytes=64)
+        nc.vector.tensor_tensor(
+            z2_bf[:].rearrange("p (c i k) -> p c k i", i=4, k=R),
+            diff[:].rearrange("p k (c i) -> p c k i", i=4),
+            gb3[:].unsqueeze(1).unsqueeze(3).to_broadcast([P, V // 4, R, 4]),
+            ALU.mult,
+        )
+        z2_w = keep.tile([P, V], U32, name="z2_w", align_bytes=64)
+        z2_s = keep.tile([P, V], U8, name="z2_s", align_bytes=64)
+        nc.vector.quantize_mx(out=z2_w[:].bitcast(FP8X4), scales=z2_s[:], in_=z2_bf[:])
+
+        top2 = keep.tile([P, R], F32, name="top2")
+        s_bias = keep.tile([P, R], F32, name="s_bias")
+        total = keep.tile([P, R, V], F32, name="total")
+        for t in range(R):
+            s_ps = psum.tile([P, V], F32, name="s_ps%d" % t, tag="narrow%d" % t)
+            nc.tensor.matmul_mx(
+                out=s_ps[:],
+                lhsT=z_w[:, P * t : P * (t + 1)].bitcast(FP8X4),
+                lhsT_scale=z_s[:, P * t : P * (t + 1)],
+                rhs=z2_w[:].bitcast(FP8X4),
+                rhs_scale=z2_s[:],
+                start=True,
+                stop=True,
+            )
+            nc.vector.tensor_scalar(
+                bs_win[t][:, :V], s_ps[:], 0.0625, None, ALU.mult, ALU.max, accum_out=top2[:, t : t + 1]
+            )
+            nc.vector.tensor_scalar(
+                s_bias[:, t : t + 1], top2[:, t : t + 1], tau3_t[:, t : t + 1], -1.0, ALU.mult, ALU.mult
+            )
+            ea3 = ring.tile([P, V], F32, name="ea3")
+            ea4 = ring.tile([P, V], F32, name="ea4")
+            nc.scalar.activation(
+                ea3[:], bs_win[t][:].indirect(n5_l[:]), ACT.Exp, bias=s_bias[:, t : t + 1], scale=tau3_t[:, t : t + 1]
+            )
+            nc.scalar.activation(
+                ea4[:], bs_win[t][:].indirect(n6_l[:]), ACT.Exp, bias=s_bias[:, t : t + 1], scale=tau3_t[:, t : t + 1]
+            )
+            nc.vector.tensor_tensor(total[:, t, :], ea3[:], ea4[:], ALU.add)
+
+        logs = keep.tile([P, R, V], F32, name="logs")
+        result = keep.tile([P, R, V], F32, name="result")
+        out_rows = out_0.rearrange("(p t) v -> p t v", t=R)
+        halves = [slice(0, V // 2), slice(V // 2, V)]
+        for cols in halves:
+            nc.scalar.activation(logs[:, :, cols], total[:, :, cols], ACT.Ln, bias=0.25)
+        result_bf = keep.tile([P, R * V], BF16, name="result_bf", align_bytes=64)
+        for cols in halves:
+            for t in range(R):
+                nc.vector.tensor_tensor(result[:, t, cols], logs[:, t, cols], bs_win[t][:, cols], ALU.add)
+            nc.sync.dma_start(out_rows[:, :, cols], result[:, :, cols])
+            round_copy = nc.scalar.copy if cols.start == 0 else nc.vector.tensor_copy
+            round_copy(
+                result_bf[:, R * cols.start : R * cols.stop].rearrange("p (c i k) -> p c k i", i=4, k=R),
+                result[:, :, cols].rearrange("p k (c i) -> p c k i", i=4),
+            )
+        out_w = keep.tile([P, V], U32, name="out_w", align_bytes=64)
+        out_s = keep.tile([P, V], U8, name="out_s", align_bytes=64)
+        nc.vector.quantize_mx(out=out_w[:].bitcast(FP8X4), scales=out_s[:], in_=result_bf[:])
+        nc.sync.dma_start(out_1[0].rearrange("p n t -> p (n t)").bitcast(I32), out_w[:].bitcast(I32))
+        for q in range(4):
+            queue = nc.scalar if q % 2 == 0 else nc.sync
+            queue.dma_start(out_2[0][4 * q : 4 * q + 4, :].bitcast(I32), out_s[32 * q : 32 * q + 4, :].bitcast(I32))

@@ -27,7 +27,7 @@ def tile_picked_hkqehpetwelg_none_po_kernel(
     nc = tc.nc
     with ExitStack() as ctx:
         keep = ctx.enter_context(tc.tile_pool(name="keep", bufs=1))
-        ring = ctx.enter_context(tc.tile_pool(name="ring", bufs=2))
+        ring = ctx.enter_context(tc.tile_pool(name="ring", bufs=4))
         stage = ctx.enter_context(tc.tile_pool(name="stage", bufs=1))
         psum = ctx.enter_context(tc.psum_pool(name="psum", bufs=1))
 
@@ -36,37 +36,40 @@ def tile_picked_hkqehpetwelg_none_po_kernel(
             nc.sync.dma_start(dst[:], src)
             return dst
 
-        def load_rows(queue, src, name, pool=keep, offset=None):
-            dst = pool.tile([P, R], F32, name=name, offset=offset)
+        def load_rows(queue, src, dst):
             queue.dma_start(dst[:], src.rearrange("(p t) o -> p (t o)", t=R))
             return dst
 
-        def load_weight_scales(dst, src, quadrants):
-            for q in quadrants:
-                rows = src[0][4 * q : 4 * q + 4, :].bitcast(I32)
-                nc.sync.dma_start(dst[32 * q : 32 * q + 32, :].bitcast(I32), rows.unsqueeze(0).to_broadcast([8, 4, H // 4]))
+        def load_weight_words(src, name):
+            dst = keep.tile([P, 2 * H], U8, name=name)
+            nc.sync.dma_start(dst[:].bitcast(I32), src[0].bitcast(I32))
+            return dst
 
-        offs_l = load_list(offs, "offs_l")
+        def load_scale_rows(dst, src):
+            nc.scalar.dma_start(dst.bitcast(I32), src[0].bitcast(I32))
+
         xs = stage.tile([P, T], U8, name="xs", offset=0)
-        for par in range(2):
-            rows = x_scales[0][par:16:2, :].bitcast(I32)
-            nc.sync.dma_start(xs[par:P:2, :].bitcast(I32), rows.unsqueeze(1).to_broadcast([8, 8, T // 4]))
+        nc.gpsimd.memset(xs[:].bitcast(I32), 0)
+        ws_raw = keep.tile([P, 2, H], U8, name="ws_raw")
+        nc.gpsimd.memset(ws_raw[:].rearrange("p j c -> p (j c)").bitcast(I32), 0)
+        load_scale_rows(xs[0:P:8, :], x_scales)
+        load_scale_rows(ws_raw[0:P:8, 0, :], w1_scales)
+        load_scale_rows(ws_raw[0:P:8, 1, :], w2_scales)
+        offs_l = load_list(offs, "offs_l")
         two_l = load_list(two, "two_l")
-        w1w_raw = keep.tile([P, 2 * H], U8, name="w1w_raw")
-        nc.sync.dma_start(w1w_raw[:].bitcast(I32), w1_words[0].bitcast(I32))
-        w1s_raw = keep.tile([P, H], U8, name="w1s_raw")
-        load_weight_scales(w1s_raw, w1_scales, (0, 1))
+        w1w_raw = load_weight_words(w1_words, "w1w_raw")
+        w2w_raw = load_weight_words(w2_words, "w2w_raw")
+        n1_l = load_list(n1, "n1_l")
         xw = keep.tile([P, T], U32, name="xw")
         nc.sync.dma_start(xw[:].bitcast(I32), x_words[0].rearrange("p n t -> p (n t)").bitcast(I32))
-        load_weight_scales(w1s_raw, w1_scales, (2, 3))
-        n1_l = load_list(n1, "n1_l")
+        ga_t = load_rows(nc.sync, ga, keep.tile([P, R], F32, name="ga_t"))
         n2_l = load_list(n2, "n2_l")
-        sl_t = load_rows(nc.gpsimd, sl, "sl_t")
-        th_t = load_rows(nc.gpsimd, th, "th_t")
         n3_l = load_list(n3, "n3_l")
         n4_l = load_list(n4, "n4_l")
         n5_l = load_list(n5, "n5_l")
         n6_l = load_list(n6, "n6_l")
+        sl_t = load_rows(nc.gpsimd, sl, keep.tile([P, R], F32, name="sl_t"))
+        th_t = load_rows(nc.gpsimd, th, keep.tile([P, R], F32, name="th_t"))
 
         a_win = [keep.tile([P, 2 * S], F32, name="a_win%d" % t) for t in range(R)]
         bs_win = [keep.tile([P, 2 * V], F32, name="bs_win%d" % t) for t in range(R)]
@@ -78,61 +81,44 @@ def tile_picked_hkqehpetwelg_none_po_kernel(
 
         def deal_words(raw, name):
             dealt = keep.tile([P, 2 * H], U8, name=name, align_bytes=64)
-            nc.gpsimd.tensor_copy(
-                dealt[:].rearrange("p (t m b) -> p t m b", t=R, b=2),
-                raw[:].rearrange("p (m t b) -> p t m b", t=R, b=2),
-            )
-            return dealt
-
-        def deal_scales(engine, raw, name):
-            dealt = keep.tile([P, H], U8, name=name, align_bytes=64)
-            engine.tensor_copy(
-                dealt[:].rearrange("p (t m) -> p t m", t=R), raw[:].rearrange("p (m t) -> p t m", t=R)
+            nc.scalar.copy(
+                dealt[:].bitcast(U16).rearrange("p (t m) -> p t m", t=R),
+                raw[:].bitcast(U16).rearrange("p (m t) -> p t m", t=R),
             )
             return dealt
 
         picked_s = keep.tile([P, S + V], U8, name="picked_s", align_bytes=64)
         nc.vector.tensor_copy(picked_s[:, :S], xs[:].indirect(offs_l[:]))
         nc.vector.tensor_copy(picked_s[:, S:], xs[:].indirect(two_l[:]))
-        plane_s = keep.tile([P, S + V], U8, name="plane_s", align_bytes=64)
-        nc.vector.tensor_copy(plane_s[:].bitcast(I32), picked_s[:].bitcast(I32))
-        for par in range(2):
-            nc.scalar.dma_start(plane_s[2 + par : P : 32, :].bitcast(I32), picked_s[16 + par : P : 32, :].bitcast(I32))
-        xa_s = plane_s[:, :S]
-        xb_s = plane_s[:, S:]
+        planes = keep.tile([P, 2 * H + S + V], U8, name="planes", align_bytes=64)
+        w1s, w2s = planes[:, :H], planes[:, H : 2 * H]
+        xa_s, xb_s = planes[:, 2 * H : 2 * H + S], planes[:, 2 * H + S :]
+        for j, dealt_s in enumerate((w1s, w2s)):
+            nc.gpsimd.tensor_copy(
+                dealt_s.rearrange("p (t m) -> p t m", t=R), ws_raw[:, j, :].rearrange("p (m t) -> p t m", t=R)
+            )
+        nc.vector.tensor_copy(planes[:, 2 * H :].bitcast(I32), picked_s[:].bitcast(I32))
         w1w = deal_words(w1w_raw, "w1w")
-        w1s = deal_scales(nc.gpsimd, w1s_raw, "w1s")
+        w2w = deal_words(w2w_raw, "w2w")
+        for i in range(1, 4):
+            nc.scalar.dma_start(planes[i:P:32, :].bitcast(I32), planes[8 * i : P : 32, :].bitcast(I32))
         xa_w = pick_words(offs_l, S, "xa_w")
         xb_w = pick_words(two_l, V, "xb_w")
         for t in range(R):
             nc.vector.memset(a_win[t][:, S:], 0.0)
             nc.vector.memset(bs_win[t][:, V:], 0.0)
 
-        ga_t = load_rows(nc.sync, ga, "ga_t", stage, 1536)
-        w2w_raw = stage.tile([P, 2 * H], U8, name="w2w_raw", offset=0)
-        nc.sync.dma_start(w2w_raw[:].bitcast(I32), w2_words[0].bitcast(I32))
-        w2s_raw = stage.tile([P, H], U8, name="w2s_raw", offset=1024)
-        load_weight_scales(w2s_raw, w2_scales, range(4))
-        tau_t = load_rows(nc.sync, tau, "tau_t", stage, 1568)
-        tau2_t = load_rows(nc.sync, tau2, "tau2_t", stage, 1600)
-        gb_t = load_rows(nc.sync, gb, "gb_t", stage, 1632)
-        tau3_t = load_rows(nc.sync, tau3, "tau3_t", stage, 1664)
-        w2w = deal_words(w2w_raw, "w2w")
-        w2s = deal_scales(nc.gpsimd, w2s_raw, "w2s")
-
-        sig_bias = stage.tile([P, R], F32, name="sig_bias", offset=1696)
+        late = [stage.tile([P, R], F32, name="late%d" % j, offset=32 * j) for j in range(5)]
+        tau_t, tau2_t, gb_t, tau3_t = [load_rows(nc.sync, src, dst) for src, dst in zip((tau, tau2, gb, tau3), late)]
+        sig_bias = late[4]
         nc.vector.scalar_tensor_tensor(sig_bias[:], sl_t[:], -1.0, th_t[:], ALU.mult, ALU.mult)
-        half_ga = keep.tile([P, R], F32, name="half_ga")
-        nc.gpsimd.tensor_scalar(half_ga[:], ga_t[:], -0.5, 0.0, ALU.mult, ALU.add)
-        gb3 = keep.tile([P, R], F32, name="gb3")
-        nc.gpsimd.tensor_scalar(gb3[:], gb_t[:], 3.0, 0.0, ALU.mult, ALU.add)
 
         def project(bank, words, scales, t, x_w, x_s):
             nc.tensor.matmul_mx(
                 out=bank,
                 lhsT=words[:, 2 * P * t : 2 * P * (t + 1)].bitcast(FP4X4),
                 lhsT_scale=scales[:, P * t : P * (t + 1)],
-                rhs=x_w[:].bitcast(FP8X4),
+                rhs=x_w.bitcast(FP8X4),
                 rhs_scale=x_s,
                 start=True,
                 stop=True,
@@ -142,18 +128,6 @@ def tile_picked_hkqehpetwelg_none_po_kernel(
         z = keep.tile([P, R, S], F32, name="z")
         whole = [keep.tile([P, S], F32, name="whole%d" % t) for t in range(R)]
 
-        a_plain = []
-
-        def product_a(t):
-            a_ps = psum.tile([P, S], F32, name="a_ps%d" % t, tag="wide%d" % (t % 2))
-            project(a_ps[:], w1w, w1s, t, xa_w, xa_s)
-            if t < 2:
-                nc.vector.tensor_copy(a_win[t][:, :S], a_ps[:])
-                a_plain.append(a_win[t][:, :S])
-            else:
-                nc.scalar.copy(a_win[t][:, :S], a_ps[:])
-                a_plain.append(a_ps[:])
-
         def gate(t):
             nc.scalar.activation(
                 st_win[t][:, S:], a_win[t][:].indirect(n1_l[:]), ACT.Sigmoid,
@@ -162,73 +136,114 @@ def tile_picked_hkqehpetwelg_none_po_kernel(
 
         def weigh(t):
             nc.vector.scalar_tensor_tensor(
-                st_win[t][:, :S], a_plain[t], half_ga[:, t : t + 1], st_win[t][:, S:], ALU.mult, ALU.mult
+                st_win[t][:, :S], a_plain[t], ga_t[:, t : t + 1], st_win[t][:, S:], ALU.mult, ALU.mult
             )
 
         def double(t):
-            nc.vector.tensor_scalar(whole[t][:], st_win[t][:, :S], -2.0, None, ALU.mult)
+            nc.vector.tensor_scalar(whole[t][:], st_win[t][:, :S], 2.0, None, ALU.mult)
 
         def fetch(t):
-            nc.vector.tensor_tensor(z[:, t, :], st_win[t][:].indirect(n2_l[:]), whole[t][:], ALU.add)
+            nc.vector.tensor_tensor(z[:, t, :], st_win[t][:].indirect(n2_l[:]), whole[t][:], ALU.subtract)
 
-        product_a(0)
-        product_a(1)
+        for h in range(2):
+            cols = slice(h * S // 2, (h + 1) * S // 2)
+            a_ps = psum.tile([P, S // 2], F32, name="a_ps0%d" % h, tag="wide%d" % h)
+            project(a_ps[:], w1w, w1s, 0, xa_w[:, cols], xa_s[:, cols])
+            nc.vector.tensor_copy(a_win[0][:, cols], a_ps[:])
+        a_plain = [a_win[0][:, :S]]
+
+        def product_a(t):
+            a_ps = psum.tile([P, S], F32, name="a_ps%d" % t, tag="wide%d" % ((t + 1) % 2))
+            project(a_ps[:], w1w, w1s, t, xa_w[:], xa_s)
+            nc.scalar.copy(a_win[t][:, :S], a_ps[:])
+            a_plain.append(a_win[t][:, :S] if t == 1 else a_ps[:])
+
         gate(0)
-        gate(1)
+        product_a(1)
         product_a(2)
-        gate(2)
+        gate(1)
         product_a(3)
+        gate(2)
         gate(3)
 
-        weigh(0)
-        double(0)
-        weigh(1)
-        fetch(0)
         top = keep.tile([P, R], F32, name="top")
         for t in range(R):
             b_ps = psum.tile([P, V], F32, name="b_ps%d" % t, tag="narrow%d" % t)
-            project(b_ps[:], w2w, w2s, t, xb_w, xb_s)
+            project(b_ps[:], w2w, w2s, t, xb_w[:], xb_s)
             nc.vector.tensor_scalar(bs_win[t][:, :V], b_ps[:], 1.0, None, ALU.mult, ALU.max, accum_out=top[:, t : t + 1])
+        weigh(0)
         exp_bias = keep.tile([P, 2, R], F32, name="exp_bias")
         nc.vector.scalar_tensor_tensor(exp_bias[:, 0, :], top[:], -1.0, tau_t[:], ALU.mult, ALU.mult)
         nc.vector.scalar_tensor_tensor(exp_bias[:, 1, :], top[:], -1.0, tau2_t[:], ALU.mult, ALU.mult)
-        for t in range(1, R):
-            double(t)
-            if t + 1 < R:
-                weigh(t + 1)
-            fetch(t)
 
-        z_bf = keep.tile([P, R * S], BF16, name="z_bf", align_bytes=64)
-        nc.vector.tensor_copy(
-            z_bf[:].rearrange("p (u m k) -> p m k u", u=R, k=R), z[:].rearrange("p k (m u) -> p m k u", u=R)
-        )
+        eas = keep.tile([P, R, 2, V], F32, name="eas", tag="a_win3")
+        second = keep.tile([P, R, V], F32, name="second")
+        z2 = keep.tile([P, R, V], F32, name="z2")
+        for t in range(R):
+            nc.scalar.activation(
+                eas[:, t, 1, :], bs_win[t][:].indirect(n4_l[:]), ACT.Exp,
+                bias=exp_bias[:, 1, t : t + 1], scale=tau2_t[:, t : t + 1],
+            )
+            nc.scalar.activation(
+                eas[:, t, 0, :], bs_win[t][:].indirect(n3_l[:]), ACT.Exp,
+                bias=exp_bias[:, 0, t : t + 1], scale=tau_t[:, t : t + 1],
+            )
+
+        def weigh_second(t):
+            nc.vector.tensor_scalar(second[:, t, :], eas[:, t, 1, :], gb_t[:, t : t + 1], None, ALU.mult)
+
+        def difference(t):
+            nc.vector.scalar_tensor_tensor(
+                z2[:, t, :], eas[:, t, 0, :], gb_t[:, t : t + 1], second[:, t, :], ALU.mult, ALU.subtract
+            )
+
+        double(0)
+        weigh(1)
+        fetch(0)
+        double(1)
+        weigh(2)
+        fetch(1)
+        double(2)
+        weigh(3)
+        fetch(2)
+        double(3)
+        for t in range(2):
+            weigh_second(t)
+        for t in range(2):
+            difference(t)
+        fetch(3)
+
+        z_bf = [keep.tile([P, R * S // 2], BF16, name="z_bf%d" % h, align_bytes=64) for h in range(2)]
         z_w = keep.tile([P, S], U32, name="z_w", align_bytes=64)
         z_s = keep.tile([P, S], U8, name="z_s", align_bytes=64)
-        nc.vector.quantize_mx(out=z_w[:].bitcast(FP8X4), scales=z_s[:], in_=z_bf[:])
+        z_cols = z[:].rearrange("p k (m u) -> p m k u", u=R)
 
-        diff = keep.tile([P, R, V], F32, name="diff")
-        eas = keep.tile([P, R, 2, V], F32, name="eas", tag="a_win3")
-        for t in range(R):
-            ea = eas[:, t, 0, :]
-            ea2 = eas[:, t, 1, :]
-            nc.scalar.activation(
-                ea, bs_win[t][:].indirect(n3_l[:]), ACT.Exp, bias=exp_bias[:, 0, t : t + 1], scale=tau_t[:, t : t + 1]
-            )
-            nc.scalar.activation(
-                ea2, bs_win[t][:].indirect(n4_l[:]), ACT.Exp, bias=exp_bias[:, 1, t : t + 1], scale=tau2_t[:, t : t + 1]
-            )
-            nc.vector.tensor_tensor(diff[:, t, :], ea, ea2, ALU.subtract)
+        def dealt(h):
+            return z_bf[h][:].rearrange("p (u m k) -> p m k u", u=2, k=R)
+
+        def quantise_z(h):
+            cols = slice(h * S // 2, (h + 1) * S // 2)
+            nc.vector.quantize_mx(out=z_w[:, cols].bitcast(FP8X4), scales=z_s[:, cols], in_=z_bf[h][:])
+
+        nc.scalar.activation(dealt(1), z_cols[:, :, :, 2:4], ACT.Copy, scale=-0.5)
+        for t in range(2, R):
+            weigh_second(t)
+        for t in range(2, R):
+            difference(t)
+        nc.vector.tensor_scalar(dealt(0), z_cols[:, :, :, 0:2], -0.5, None, ALU.mult)
         z2_bf = keep.tile([P, R * V], BF16, name="z2_bf", align_bytes=64)
-        nc.vector.tensor_tensor(
+        nc.vector.tensor_scalar(
             z2_bf[:].rearrange("p (c i k) -> p c k i", i=4, k=R),
-            diff[:].rearrange("p k (c i) -> p c k i", i=4),
-            gb3[:].unsqueeze(1).unsqueeze(3).to_broadcast([P, V // 4, R, 4]),
-            ALU.mult,
+            z2[:].rearrange("p k (c i) -> p c k i", i=4),
+            3.0, None, ALU.mult,
         )
+        quantise_z(0)
         z2_w = keep.tile([P, V], U32, name="z2_w", align_bytes=64)
         z2_s = keep.tile([P, V], U8, name="z2_s", align_bytes=64)
         nc.vector.quantize_mx(out=z2_w[:].bitcast(FP8X4), scales=z2_s[:], in_=z2_bf[:])
+        quantise_z(1)
 
+        s_all = keep.tile([P, R, V], F32, name="s_all")
         top2 = keep.tile([P, R], F32, name="top2")
         s_bias = keep.tile([P, R], F32, name="s_bias")
         total = keep.tile([P, R, V], F32, name="total")
@@ -257,6 +272,7 @@ def tile_picked_hkqehpetwelg_none_po_kernel(
             nc.scalar.activation(
                 ea4[:], bs_win[t][:].indirect(n6_l[:]), ACT.Exp, bias=s_bias[:, t : t + 1], scale=tau3_t[:, t : t + 1]
             )
+            nc.vector.tensor_copy(s_all[:, t, :], bs_win[t][:, :V])
             nc.vector.tensor_tensor(total[:, t, :], ea3[:], ea4[:], ALU.add)
 
         logs = keep.tile([P, R, V], F32, name="logs")
@@ -267,8 +283,7 @@ def tile_picked_hkqehpetwelg_none_po_kernel(
             nc.scalar.activation(logs[:, :, cols], total[:, :, cols], ACT.Ln, bias=0.25)
         result_bf = keep.tile([P, R * V], BF16, name="result_bf", align_bytes=64)
         for cols in halves:
-            for t in range(R):
-                nc.vector.tensor_tensor(result[:, t, cols], logs[:, t, cols], bs_win[t][:, cols], ALU.add)
+            nc.vector.tensor_tensor(result[:, :, cols], logs[:, :, cols], s_all[:, :, cols], ALU.add)
             nc.sync.dma_start(out_rows[:, :, cols], result[:, :, cols])
             round_copy = nc.scalar.copy if cols.start == 0 else nc.vector.tensor_copy
             round_copy(

from contextlib import ExitStack

import concourse.mybir as mybir

K, T, S, V, H = 512, 2048, 512, 256, 512
FLOPS = 2 * K * H * S + 2 * K * H * V + 2 * H * S * V

F32 = mybir.dt.float32
BF16 = mybir.dt.bfloat16
I32 = mybir.dt.int32
U32 = mybir.dt.uint32
U16 = mybir.dt.uint16
U8 = mybir.dt.uint8
FP8X4 = mybir.dt.float8_e4m3fn_x4
FP4X4 = mybir.dt.float4_e2m1fn_x4
ALU = mybir.AluOpType
ACT = mybir.ActivationFunctionType

P = 128
R = 4


def tile_picked_hkqehpetwelg_none_po_kernel(
    tc, x_words, x_scales, w1_words, w1_scales, w2_words, w2_scales, sl, th, tau, tau2, ga, gb, tau3,
    offs, two, n1, n2, n3, n4, n5, n6, out_0, out_1, out_2,
):
    nc = tc.nc
    with ExitStack() as ctx:
        keep = ctx.enter_context(tc.tile_pool(name="keep", bufs=1))
        ring = ctx.enter_context(tc.tile_pool(name="ring", bufs=4))
        stage = ctx.enter_context(tc.tile_pool(name="stage", bufs=1))
        psum = ctx.enter_context(tc.psum_pool(name="psum", bufs=1))

        def load_list(src, name):
            dst = keep.tile(list(src.shape), U16, name=name)
            nc.sync.dma_start(dst[:], src)
            return dst

        def load_rows(queue, src, dst):
            queue.dma_start(dst[:], src.rearrange("(p t) o -> p (t o)", t=R))
            return dst

        def load_weight_words(src, name):
            dst = keep.tile([P, 2 * H], U8, name=name)
            nc.sync.dma_start(dst[:].bitcast(I32), src[0].bitcast(I32))
            return dst

        def load_scale_rows(dst, src):
            nc.scalar.dma_start(dst.bitcast(I32), src[0].bitcast(I32))

        xs = stage.tile([P, T], U8, name="xs", offset=0)
        nc.gpsimd.memset(xs[:].bitcast(I32), 0)
        ws_raw = keep.tile([P, 2, H], U8, name="ws_raw")
        nc.gpsimd.memset(ws_raw[:].rearrange("p j c -> p (j c)").bitcast(I32), 0)
        load_scale_rows(xs[0:P:8, :], x_scales)
        load_scale_rows(ws_raw[0:P:8, 0, :], w1_scales)
        load_scale_rows(ws_raw[0:P:8, 1, :], w2_scales)
        offs_l = load_list(offs, "offs_l")
        two_l = load_list(two, "two_l")
        w1w_raw = load_weight_words(w1_words, "w1w_raw")
        w2w_raw = load_weight_words(w2_words, "w2w_raw")
        n1_l = load_list(n1, "n1_l")
        xw = keep.tile([P, T], U32, name="xw")
        nc.sync.dma_start(xw[:].bitcast(I32), x_words[0].rearrange("p n t -> p (n t)").bitcast(I32))
        ga_t = load_rows(nc.sync, ga, keep.tile([P, R], F32, name="ga_t"))
        n2_l = load_list(n2, "n2_l")
        n3_l = load_list(n3, "n3_l")
        n4_l = load_list(n4, "n4_l")
        n5_l = load_list(n5, "n5_l")
        n6_l = load_list(n6, "n6_l")
        sl_t = load_rows(nc.gpsimd, sl, keep.tile([P, R], F32, name="sl_t"))
        th_t = load_rows(nc.gpsimd, th, keep.tile([P, R], F32, name="th_t"))

        a_win = [keep.tile([P, 2 * S], F32, name="a_win%d" % t) for t in range(R)]
        bs_win = [keep.tile([P, 2 * V], F32, name="bs_win%d" % t) for t in range(R)]

        def pick_words(lst, n, name):
            picked = keep.tile([P, n], U32, name=name, align_bytes=64)
            nc.vector.tensor_copy(picked[:], xw[:].indirect(lst[:]))
            return picked

        def deal_words(raw, name):
            dealt = keep.tile([P, 2 * H], U8, name=name, align_bytes=64)
            nc.scalar.copy(
                dealt[:].bitcast(U16).rearrange("p (t m) -> p t m", t=R),
                raw[:].bitcast(U16).rearrange("p (m t) -> p t m", t=R),
            )
            return dealt

        picked_s = keep.tile([P, S + V], U8, name="picked_s", align_bytes=64)
        nc.vector.tensor_copy(picked_s[:, :S], xs[:].indirect(offs_l[:]))
        nc.vector.tensor_copy(picked_s[:, S:], xs[:].indirect(two_l[:]))
        planes = keep.tile([P, 2 * H + S + V], U8, name="planes", align_bytes=64)
        w1s, w2s = planes[:, :H], planes[:, H : 2 * H]
        xa_s, xb_s = planes[:, 2 * H : 2 * H + S], planes[:, 2 * H + S :]
        for j, dealt_s in enumerate((w1s, w2s)):
            nc.gpsimd.tensor_copy(
                dealt_s.rearrange("p (t m) -> p t m", t=R), ws_raw[:, j, :].rearrange("p (m t) -> p t m", t=R)
            )
        nc.vector.tensor_copy(planes[:, 2 * H :].bitcast(I32), picked_s[:].bitcast(I32))
        w1w = deal_words(w1w_raw, "w1w")
        w2w = deal_words(w2w_raw, "w2w")
        for i in range(1, 4):
            nc.scalar.dma_start(planes[i:P:32, :].bitcast(I32), planes[8 * i : P : 32, :].bitcast(I32))
        xa_w = pick_words(offs_l, S, "xa_w")
        xb_w = pick_words(two_l, V, "xb_w")
        for t in range(R):
            nc.vector.memset(a_win[t][:, S:], 0.0)
            nc.vector.memset(bs_win[t][:, V:], 0.0)

        late = [stage.tile([P, R], F32, name="late%d" % j, offset=32 * j) for j in range(5)]
        tau_t, tau2_t, gb_t, tau3_t = [load_rows(nc.sync, src, dst) for src, dst in zip((tau, tau2, gb, tau3), late)]
        sig_bias = late[4]
        nc.vector.scalar_tensor_tensor(sig_bias[:], sl_t[:], -1.0, th_t[:], ALU.mult, ALU.mult)

        def project(bank, words, scales, t, x_w, x_s):
            nc.tensor.matmul_mx(
                out=bank,
                lhsT=words[:, 2 * P * t : 2 * P * (t + 1)].bitcast(FP4X4),
                lhsT_scale=scales[:, P * t : P * (t + 1)],
                rhs=x_w.bitcast(FP8X4),
                rhs_scale=x_s,
                start=True,
                stop=True,
            )

        st_win = [keep.tile([P, 2 * S], F32, name="st_win%d" % t) for t in range(R)]
        z = keep.tile([P, R, S], F32, name="z")
        whole = [keep.tile([P, S], F32, name="whole%d" % t) for t in range(R)]

        def gate(t):
            nc.scalar.activation(
                st_win[t][:, S:], a_win[t][:].indirect(n1_l[:]), ACT.Sigmoid,
                bias=sig_bias[:, t : t + 1], scale=sl_t[:, t : t + 1],
            )

        def weigh(t):
            nc.vector.scalar_tensor_tensor(
                st_win[t][:, :S], a_plain[t], ga_t[:, t : t + 1], st_win[t][:, S:], ALU.mult, ALU.mult
            )

        def double(t):
            nc.vector.tensor_scalar(whole[t][:], st_win[t][:, :S], 2.0, None, ALU.mult)

        def fetch(t):
            nc.vector.tensor_tensor(z[:, t, :], st_win[t][:].indirect(n2_l[:]), whole[t][:], ALU.subtract)

        for h in range(2):
            cols = slice(h * S // 2, (h + 1) * S // 2)
            a_ps = psum.tile([P, S // 2], F32, name="a_ps0%d" % h, tag="wide%d" % h)
            project(a_ps[:], w1w, w1s, 0, xa_w[:, cols], xa_s[:, cols])
            nc.vector.tensor_copy(a_win[0][:, cols], a_ps[:])
        a_plain = [a_win[0][:, :S]]

        def product_a(t):
            a_ps = psum.tile([P, S], F32, name="a_ps%d" % t, tag="wide%d" % ((t + 1) % 2))
            project(a_ps[:], w1w, w1s, t, xa_w[:], xa_s)
            nc.scalar.copy(a_win[t][:, :S], a_ps[:])
            a_plain.append(a_win[t][:, :S] if t == 1 else a_ps[:])

        gate(0)
        product_a(1)
        product_a(2)
        gate(1)
        product_a(3)
        gate(2)
        gate(3)

        top = keep.tile([P, R], F32, name="top")
        for t in range(R):
            b_ps = psum.tile([P, V], F32, name="b_ps%d" % t, tag="narrow%d" % t)
            project(b_ps[:], w2w, w2s, t, xb_w[:], xb_s)
            nc.vector.tensor_scalar(bs_win[t][:, :V], b_ps[:], 1.0, None, ALU.mult, ALU.max, accum_out=top[:, t : t + 1])
        weigh(0)
        exp_bias = keep.tile([P, 2, R], F32, name="exp_bias")
        nc.vector.scalar_tensor_tensor(exp_bias[:, 0, :], top[:], -1.0, tau_t[:], ALU.mult, ALU.mult)
        nc.vector.scalar_tensor_tensor(exp_bias[:, 1, :], top[:], -1.0, tau2_t[:], ALU.mult, ALU.mult)

        eas = keep.tile([P, R, 2, V], F32, name="eas", tag="a_win3")
        second = keep.tile([P, R, V], F32, name="second")
        z2 = keep.tile([P, R, V], F32, name="z2")
        for t in range(R):
            nc.scalar.activation(
                eas[:, t, 1, :], bs_win[t][:].indirect(n4_l[:]), ACT.Exp,
                bias=exp_bias[:, 1, t : t + 1], scale=tau2_t[:, t : t + 1],
            )
            nc.scalar.activation(
                eas[:, t, 0, :], bs_win[t][:].indirect(n3_l[:]), ACT.Exp,
                bias=exp_bias[:, 0, t : t + 1], scale=tau_t[:, t : t + 1],
            )

        def weigh_second(t):
            nc.vector.tensor_scalar(second[:, t, :], eas[:, t, 1, :], gb_t[:, t : t + 1], None, ALU.mult)

        def difference(t):
            nc.vector.scalar_tensor_tensor(
                z2[:, t, :], eas[:, t, 0, :], gb_t[:, t : t + 1], second[:, t, :], ALU.mult, ALU.subtract
            )

        double(0)
        weigh(1)
        fetch(0)
        double(1)
        weigh(2)
        fetch(1)
        double(2)
        weigh(3)
        fetch(2)
        double(3)
        for t in range(2):
            weigh_second(t)
        for t in range(2):
            difference(t)
        fetch(3)

        z_bf = [keep.tile([P, R * S // 2], BF16, name="z_bf%d" % h, align_bytes=64) for h in range(2)]
        z_w = keep.tile([P, S], U32, name="z_w", align_bytes=64)
        z_s = keep.tile([P, S], U8, name="z_s", align_bytes=64)
        z_cols = z[:].rearrange("p k (m u) -> p m k u", u=R)

        def dealt(h):
            return z_bf[h][:].rearrange("p (u m k) -> p m k u", u=2, k=R)

        def quantise_z(h):
            cols = slice(h * S // 2, (h + 1) * S // 2)
            nc.vector.quantize_mx(out=z_w[:, cols].bitcast(FP8X4), scales=z_s[:, cols], in_=z_bf[h][:])

        nc.scalar.activation(dealt(1), z_cols[:, :, :, 2:4], ACT.Copy, scale=-0.5)
        for t in range(2, R):
            weigh_second(t)
        for t in range(2, R):
            difference(t)
        nc.vector.tensor_scalar(dealt(0), z_cols[:, :, :, 0:2], -0.5, None, ALU.mult)
        z2_bf = keep.tile([P, R * V], BF16, name="z2_bf", align_bytes=64)
        nc.vector.tensor_scalar(
            z2_bf[:].rearrange("p (c i k) -> p c k i", i=4, k=R),
            z2[:].rearrange("p k (c i) -> p c k i", i=4),
            3.0, None, ALU.mult,
        )
        quantise_z(0)
        z2_w = keep.tile([P, V], U32, name="z2_w", align_bytes=64)
        z2_s = keep.tile([P, V], U8, name="z2_s", align_bytes=64)
        nc.vector.quantize_mx(out=z2_w[:].bitcast(FP8X4), scales=z2_s[:], in_=z2_bf[:])
        quantise_z(1)

        s_all = keep.tile([P, R, V], F32, name="s_all")
        top2 = keep.tile([P, R], F32, name="top2")
        s_bias = keep.tile([P, R], F32, name="s_bias")
        total = keep.tile([P, R, V], F32, name="total")
        for t in range(R):
            s_ps = psum.tile([P, V], F32, name="s_ps%d" % t, tag="narrow%d" % t)
            nc.tensor.matmul_mx(
                out=s_ps[:],
                lhsT=z_w[:, P * t : P * (t + 1)].bitcast(FP8X4),
                lhsT_scale=z_s[:, P * t : P * (t + 1)],
                rhs=z2_w[:].bitcast(FP8X4),
                rhs_scale=z2_s[:],
                start=True,
                stop=True,
            )
            nc.vector.tensor_scalar(
                bs_win[t][:, :V], s_ps[:], 0.0625, None, ALU.mult, ALU.max, accum_out=top2[:, t : t + 1]
            )
            nc.vector.tensor_scalar(
                s_bias[:, t : t + 1], top2[:, t : t + 1], tau3_t[:, t : t + 1], -1.0, ALU.mult, ALU.mult
            )
            ea3 = ring.tile([P, V], F32, name="ea3")
            ea4 = ring.tile([P, V], F32, name="ea4")
            nc.scalar.activation(
                ea3[:], bs_win[t][:].indirect(n5_l[:]), ACT.Exp, bias=s_bias[:, t : t + 1], scale=tau3_t[:, t : t + 1]
            )
            nc.scalar.activation(
                ea4[:], bs_win[t][:].indirect(n6_l[:]), ACT.Exp, bias=s_bias[:, t : t + 1], scale=tau3_t[:, t : t + 1]
            )
            nc.vector.tensor_copy(s_all[:, t, :], bs_win[t][:, :V])
            nc.vector.tensor_tensor(total[:, t, :], ea3[:], ea4[:], ALU.add)

        logs = keep.tile([P, R, V], F32, name="logs")
        result = keep.tile([P, R, V], F32, name="result")
        out_rows = out_0.rearrange("(p t) v -> p t v", t=R)
        halves = [slice(0, V // 2), slice(V // 2, V)]
        for cols in halves:
            nc.scalar.activation(logs[:, :, cols], total[:, :, cols], ACT.Ln, bias=0.25)
        result_bf = keep.tile([P, R * V], BF16, name="result_bf", align_bytes=64)
        for cols in halves:
            nc.vector.tensor_tensor(result[:, :, cols], logs[:, :, cols], s_all[:, :, cols], ALU.add)
            nc.sync.dma_start(out_rows[:, :, cols], result[:, :, cols])
            round_copy = nc.scalar.copy if cols.start == 0 else nc.vector.tensor_copy
            round_copy(
                result_bf[:, R * cols.start : R * cols.stop].rearrange("p (c i k) -> p c k i", i=4, k=R),
                result[:, :, cols].rearrange("p k (c i) -> p c k i", i=4),
            )
        out_w = keep.tile([P, V], U32, name="out_w", align_bytes=64)
        out_s = keep.tile([P, V], U8, name="out_s", align_bytes=64)
        nc.vector.quantize_mx(out=out_w[:].bitcast(FP8X4), scales=out_s[:], in_=result_bf[:])
        nc.sync.dma_start(out_1[0].rearrange("p n t -> p (n t)").bitcast(I32), out_w[:].bitcast(I32))
        for q in range(4):
            queue = nc.scalar if q % 2 == 0 else nc.sync
            queue.dma_start(out_2[0][4 * q : 4 * q + 4, :].bitcast(I32), out_s[32 * q : 32 * q + 4, :].bitcast(I32))
